import numpy as np
import ml_dtypes


def mxq(x, axis, fmt="e4m3"):
    dtype, down = {"e4m3": (ml_dtypes.float8_e4m3fn, 7), "e5m2": (ml_dtypes.float8_e5m2, 14)}[fmt]
    v = np.moveaxis(np.asarray(x, np.float32).astype(ml_dtypes.bfloat16).astype(np.float64), axis, -1)
    blocks = v.reshape(v.shape[:-1] + (-1, 32))
    amax = np.abs(blocks).max(-1, keepdims=True)
    byte = np.maximum(np.where(amax > 0, np.frexp(amax)[1] - 1 + 127, 0) - down, 1)
    scale = np.exp2(byte - 127.0)
    codes = (blocks / scale).astype(np.float32).astype(dtype).astype(np.float64)
    return np.moveaxis((codes * scale).reshape(v.shape), -1, axis)


WIDE = False


def mx_kscale(k):
    if not WIDE:
        return np.ones(k)
    levels = np.array([10, -10, 5, -5, 0])
    if k % 512:
        return np.exp2(np.random.permutation(np.resize(levels, k // 32))).repeat(32)
    a = np.empty((k // 512, 16))
    for p in range(k // 512):
        a[p, :8] = np.random.permutation(np.resize(levels, 8))
        for g in range(8):
            far = levels[np.abs(levels - a[p, g]) >= 10]
            a[p, g + 8] = far[np.random.randint(len(far))]
    return np.exp2(a.ravel()).repeat(32)


def f64(x):
    return np.asarray(x).astype(np.float64)


def striped(idx):
    return np.tile(idx.reshape(-1, 16).T, (8, 1)).astype(np.uint16)


def unstriped(offs):
    return offs[:16].T.reshape(-1).astype(np.int64)


def striped8(idx):
    return np.concatenate([x.reshape(-1, 16).T for x in idx]).astype(np.uint16)


def runs(offs, k):
    lists = np.stack([offs[16 * r : 16 * r + 16].T.reshape(-1) for r in range(8)]).astype(np.int64)
    return lists[np.arange(k) % 512 // 64]


def pack_weight(w):
    k, n = w.shape
    w = f64(np.asarray(w, np.float32).astype(ml_dtypes.bfloat16)).reshape(k // 32, 32, n)
    amax = np.abs(w).max(1)
    byte = np.clip(np.where(amax > 0, np.frexp(amax)[1] - 1 + 127 - 7, 1), 1, 254)
    scaled = (w * np.exp2(127.0 - byte)[:, None, :]).reshape(k, n).astype(np.float32)
    words = np.ascontiguousarray(scaled.reshape(k // 512, 128, 4, n).transpose(0, 1, 3, 2)).astype(ml_dtypes.float8_e4m3fn).view(np.uint8)
    return words, np.ascontiguousarray(byte.astype(np.uint8).reshape(k // 512, 16, n))


def unpack_weight(words, scales):
    g, p, n, _ = words.shape
    vals = np.ascontiguousarray(words).view(ml_dtypes.float8_e4m3fn).astype(np.float64) * np.repeat(np.exp2(scales.astype(np.float64) - 127.0), 8, axis=1)[..., None]
    return vals.transpose(0, 1, 3, 2).reshape(g * 512, n)


def sigmoid(v):
    return 1.0 / (1.0 + np.exp(-np.maximum(v, -700.0)))

def planes(y):
    n, m = y.shape
    v = y.astype(np.float32).astype(ml_dtypes.bfloat16).astype(np.float64).reshape(n // 32, 32, m)
    top = np.abs(v).max(1)
    byte = np.clip(np.where(top > 0, np.frexp(top)[1] - 1 + 127 - 7, 1), 1, 254)
    codes = (v * np.exp2(127.0 - byte)[:, None, :]).reshape(n, m).astype(np.float32).astype(ml_dtypes.float8_e4m3fn).view(np.uint8)
    words = codes.reshape(n // 512, 128, 4, m).transpose(0, 1, 3, 2)
    return np.ascontiguousarray(words), np.ascontiguousarray(byte.astype(np.uint8).reshape(n // 512, 16, m))


K, T, S, N, H, U = 512, 2048, 512, 512, 512, 1024


def setup_inputs():
    n = np.random.standard_normal
    s = mx_kscale(K)[:, None]
    u = mx_kscale(H)
    packed_xT = pack_weight(n((K, T)) * s)
    packed_w1 = pack_weight(n((K, H)) / np.sqrt(K) / s)
    packed_w2 = pack_weight(n((H, N)) / np.sqrt(H) / u[:, None])
    return {
        "x_words": packed_xT[0],
        "x_scales": packed_xT[1],
        "w1_words": packed_w1[0],
        "w1_scales": packed_w1[1],
        "mem": n((H, U)).astype(np.float32),
        "gn": (np.random.uniform(0.5, 1.5, (H, 1)) * u[:, None]).astype(np.float32),
        "w2_words": packed_w2[0],
        "w2_scales": packed_w2[1],
        "offs": striped(np.random.permutation(T)[:S]),
        "slot": striped8(np.stack([np.random.permutation(U)[:S] for _ in range(8)])),
        "mate": striped8(np.stack([np.random.permutation(U) for _ in range(8)])),
    }


def reference(x_words, x_scales, w1_words, w1_scales, mem, gn, w2_words, w2_scales, offs, slot, mate):
    xq = unpack_weight(x_words, x_scales)[:, unstriped(offs)]
    y = unpack_weight(w1_words, w1_scales).T @ xq
    nw = sigmoid(y) * (y - (f64(mem)[np.arange(H)[:, None], runs(slot, H)]))
    pg = f64(mem).copy()
    pg[np.arange(H)[:, None], runs(slot, H)] = nw
    z = f64(gn) * pg
    h = unpack_weight(w2_words, w2_scales).T @ mxq(z, 0, "e4m3")
    out_0 = np.minimum(h, h[np.arange(N)[:, None], runs(mate, N)])
    return (out_0,) + planes(out_0)

@@ -1,0 +1,234 @@
+from contextlib import ExitStack
+
+import concourse.mybir as mybir
+
+K, T, S, N, H, U = 512, 2048, 512, 512, 512, 1024
+FLOPS = 2 * K * H * S + 2 * H * N * U
+
+F32 = mybir.dt.float32
+BF16 = mybir.dt.bfloat16
+I32 = mybir.dt.int32
+U32 = mybir.dt.uint32
+U16 = mybir.dt.uint16
+U8 = mybir.dt.uint8
+FP8X4 = mybir.dt.float8_e4m3fn_x4
+ACT = mybir.ActivationFunctionType
+ALU = mybir.AluOpType
+
+P = 128
+PACK = 4
+QUADS = 4
+BANK = 512
+PART = 256
+PARTS = U // PART
+ORDER = (0, 2, 3, 1)
+W2_ROW = 4
+
+
+def tile_picked_pagemin_none_po_kernel(
+    tc, x_words, x_scales, w1_words, w1_scales, mem, gn, w2_words, w2_scales, offs, slot, mate, out_0, out_1, out_2
+):
+    nc = tc.nc
+
+    def words_of(dram):
+        return dram[0].rearrange("p n t -> p (n t)").bitcast(I32)
+
+    with ExitStack() as ctx:
+        keep = ctx.enter_context(tc.tile_pool(name="keep", bufs=1))
+        ring = ctx.enter_context(tc.tile_pool(name="ring", bufs=2))
+        psum = ctx.enter_context(tc.psum_pool(name="psum", bufs=8))
+
+        offs_sb = keep.tile([P, S // 16], U16, name="offs_sb")
+        slot_sb = keep.tile([P, S // 16], U16, name="slot_sb")
+        mate_sb = keep.tile([P, U // 16], U16, name="mate_sb")
+        first, second, third, last = ORDER
+        x_tab = keep.tile([P, T], U32, name="x_tab", tag="x_then_page", align_bytes=64)
+        xs_tab = keep.tile([P, T], U8, name="xs_tab", tag="xs_then_page", align_bytes=64)
+        w1_raw = keep.tile([P, H], U32, name="w1_raw", tag="w1_then_page", align_bytes=64)
+        ws_raw = keep.tile([P, H], U8, name="ws_raw", tag="ws_then_gain", align_bytes=64)
+        page = {first: keep.tile([P, U], F32, name="page_first", align_bytes=64)}
+        mem_rows = mem.rearrange("(p t) w -> p t w", t=PACK)
+
+        nc.vector.memset(xs_tab[:].bitcast(I32), 0)
+        nc.vector.memset(ws_raw[:].bitcast(I32), 0)
+
+        def load_scale_rows(queue, plane, scales, q):
+            queue.dma_start(plane[32 * q : 32 * q + 4, :].bitcast(I32), scales[0, 4 * q : 4 * q + 4, :].bitcast(I32))
+
+        nc.sync.dma_start(offs_sb[:], offs)
+        nc.sync.dma_start(slot_sb[:], slot)
+        nc.sync.dma_start(mate_sb[:], mate)
+        nc.sync.dma_start(x_tab[:].bitcast(I32), words_of(x_words))
+        nc.sync.dma_start(w1_raw[:].bitcast(I32), words_of(w1_words))
+        nc.sync.dma_start(page[first][:], mem_rows[:, first, :])
+        for q in range(QUADS):
+            load_scale_rows(nc.scalar, xs_tab, x_scales, q)
+        for q in range(QUADS):
+            load_scale_rows(nc.scalar if q < QUADS // 2 else nc.gpsimd, ws_raw, w1_scales, q)
+
+        xq = keep.tile([P, S], U32, name="xq", tag=f"old{last}", align_bytes=64)
+        xq_s = keep.tile([P, S], U8, name="xq_s", tag="xq_s_then_ws2", align_bytes=64)
+        nc.vector.tensor_copy(xq_s[:], xs_tab[:].indirect(offs_sb[:]))
+        nc.vector.tensor_copy(xq[:], x_tab[:].indirect(offs_sb[:]))
+
+        def deal(copy, raw, dtype, name, tag):
+            dealt = keep.tile([P, H], dtype, name=name, tag=tag, align_bytes=64)
+            copy(dealt[:].rearrange("p (t m) -> p m t", t=PACK), raw[:].rearrange("p (m t) -> p m t", t=PACK))
+            return dealt
+
+        ws = deal(nc.vector.tensor_copy, ws_raw, U8, "ws", "ws")
+        w1 = keep.tile([P, PACK, P], U32, name="w1", tag=f"old{third}", align_bytes=64)
+        w1_by_plane = w1_raw[:].rearrange("p (m t) -> p t m", t=PACK)
+        for t in ORDER:
+            nc.gpsimd.tensor_copy(w1[:, t, :], w1_by_plane[:, t, :])
+
+        for t, tag in ((second, "xs_then_page"), (third, "w1_then_page"), (last, "x_then_page")):
+            page[t] = keep.tile([P, U], F32, name=f"page{t}", tag=tag, align_bytes=64)
+            nc.sync.dma_start(page[t][:], mem_rows[:, t, :])
+        gain = keep.tile([P, PACK], F32, name="gain", tag="ws_then_gain", align_bytes=64)
+        nc.sync.dma_start(gain[:], gn.rearrange("(p t) o -> p (t o)", t=PACK))
+
+        y = {}
+        for t in ORDER:
+            cols = slice(t * P, (t + 1) * P)
+            y[t] = psum.tile([P, BANK], F32, name="bank")
+            nc.tensor.matmul_mx(
+                out=y[t][:], lhsT=w1[:, t, :].bitcast(FP8X4), lhsT_scale=ws[:, cols],
+                rhs=xq[:].bitcast(FP8X4), rhs_scale=xq_s[:], start=True, stop=True,
+            )
+
+        w2_raw = keep.tile([P, N], U32, name="w2_raw", tag="ws", align_bytes=64)
+        nc.sync.dma_start(w2_raw[:].bitcast(I32), words_of(w2_words))
+        ws2_raw = keep.tile([P, H], U8, name="ws2_raw", tag="xq_s_then_ws2", align_bytes=64)
+        nc.gpsimd.memset(ws2_raw[:].bitcast(I32), 0)
+        for q in range(QUADS):
+            load_scale_rows(nc.sync, ws2_raw, w2_scales, q)
+
+        z = [keep.tile([P, PART, PACK], BF16, name=f"z{c}", align_bytes=64) for c in range(PARTS)]
+        old, gate, diff = {}, {}, {}
+
+        def fetch_old(t):
+            old[t] = keep.tile([P, S], F32, name=f"old{t}", tag=f"old{first if t == second else t}", align_bytes=64)
+            if t == first:
+                nc.vector.tensor_copy(old[t][:], page[t][:].indirect(slot_sb[:]))
+            else:
+                nc.scalar.activation(old[t][:], page[t][:].indirect(slot_sb[:]), ACT.Copy)
+
+        def make_gate(t):
+            gate[t] = ring.tile([P, S], F32, name="gate", align_bytes=64)
+            nc.scalar.activation(gate[t][:], y[t][:], ACT.Sigmoid)
+
+        def make_diff(t):
+            diff[t] = keep.tile([P, S], F32, name=f"diff{t}", tag=f"diff{t}", align_bytes=64)
+            nc.vector.tensor_tensor(diff[t][:], y[t][:], old[t][:], ALU.subtract)
+
+        def scatter(t):
+            nc.vector.tensor_tensor(page[t][:].indirect(slot_sb[:]), gate[t][:], diff[t][:], ALU.mult)
+
+        def scale_on_scalar(t, c):
+            nc.scalar.activation(z[c][:, :, t], page[t][:, c * PART : (c + 1) * PART], ACT.Copy, scale=gain[:, t : t + 1])
+
+        def scale_on_vector(t, c):
+            nc.vector.tensor_scalar(z[c][:, :, t], page[t][:, c * PART : (c + 1) * PART], gain[:, t : t + 1], None, ALU.mult)
+
+        fetch_old(first)
+        make_gate(first)
+        make_diff(first)
+        scatter(first)
+        make_gate(second)
+        for t in ORDER[1:]:
+            fetch_old(t)
+        make_gate(third)
+        make_diff(second)
+        make_diff(third)
+        for c in range(PARTS):
+            scale_on_scalar(first, c)
+        scatter(second)
+        make_gate(last)
+        for c in range(PARTS):
+            scale_on_scalar(second, c)
+        scatter(third)
+        make_diff(last)
+        w2 = deal(nc.vector.tensor_copy, w2_raw, U32, "w2", f"diff{second}")
+        ws2 = deal(nc.vector.tensor_copy, ws2_raw, U8, "ws2", f"diff{third}")
+        scatter(last)
+        for c in range(PARTS):
+            scale_on_scalar(third, c)
+        for c in range(PARTS // 2):
+            scale_on_vector(last, c)
+        for c in range(PARTS // 2, PARTS):
+            scale_on_scalar(last, c)
+
+        z_codes, z_scales = [], []
+        for c in range(PARTS):
+            z_codes.append(keep.tile([P, PART], U32, name=f"z_codes{c}", tag=f"low{PARTS - 1 - c}", align_bytes=64))
+            z_scales.append(keep.tile([P, PART], U8, name=f"z_scales{c}", align_bytes=64))
+            nc.vector.quantize_mx(
+                out=z_codes[c][:].bitcast(FP8X4), scales=z_scales[c][:], in_=z[c][:].rearrange("p w t -> p (w t)")
+            )
+
+        h_bank, h = {}, []
+        for t in range(PACK):
+            cols = slice(t * P, (t + 1) * P)
+            for half in range(U // BANK):
+                h_bank[t, half] = psum.tile([P, BANK], F32, name="bank")
+                for i in range(BANK // PART):
+                    c = half * (BANK // PART) + i
+                    nc.tensor.matmul_mx(
+                        out=h_bank[t, half][:, i * PART : (i + 1) * PART], lhsT=w2[:, cols].bitcast(FP8X4),
+                        lhsT_scale=ws2[:, cols], rhs=z_codes[c][:].bitcast(FP8X4), rhs_scale=z_scales[c][:],
+                        start=True, stop=True,
+                    )
+        for t in range(PACK):
+            h.append(keep.tile([P, U], F32, name=f"h{t}", align_bytes=64))
+            for half in range(U // BANK):
+                dst = h[t][:, half * BANK : (half + 1) * BANK]
+                if half == 0:
+                    nc.scalar.copy(dst, h_bank[t, half][:])
+                else:
+                    nc.vector.tensor_copy(dst, h_bank[t, half][:])
+
+        out_rows = out_0.rearrange("(p t) w -> p t w", t=PACK)
+        out_words = words_of(out_1)
+        out_scales = keep.tile([P, U], U8, name="out_scales", align_bytes=64)
+        low, rounded = {}, {}
+
+        def take_min(t, c):
+            half, i = divmod(c, BANK // PART)
+            mated = ring.tile([P, PART], F32, name=f"mated{t}", bufs=PARTS, align_bytes=64)
+            window = h[t][:].indirect(mate_sb[:, c * PART // 16 : (c + 1) * PART // 16])
+            if (t, c) == (0, 0):
+                nc.vector.tensor_copy(mated[:], window)
+            else:
+                nc.scalar.activation(mated[:], window, ACT.Copy)
+            nc.vector.tensor_tensor(low[c][:, t, :], h_bank[t, half][:, i * PART : (i + 1) * PART], mated[:], ALU.min)
+
+        def round_part(c):
+            rounded[c] = keep.tile([P, PART, PACK], BF16, name=f"rounded{c}", align_bytes=64)
+            nc.vector.tensor_copy(
+                rounded[c][:].rearrange("p (g i) t -> p g t i", i=4), low[c][:].rearrange("p t (g i) -> p g t i", i=4)
+            )
+
+        def quantize_part(c):
+            cols = slice(c * PART, (c + 1) * PART)
+            codes = keep.tile([P, PART], U32, name=f"codes{c}", align_bytes=64)
+            nc.vector.quantize_mx(
+                out=codes[:].bitcast(FP8X4), scales=out_scales[:, cols], in_=rounded[c][:].rearrange("p w t -> p (w t)")
+            )
+            nc.sync.dma_start(out_words[:, cols], codes[:].bitcast(I32))
+
+        for c in range(PARTS):
+            low[c] = keep.tile([P, PACK, PART], F32, name=f"low{c}", tag=f"low{c}", align_bytes=64)
+            if c > 0:
+                round_part(c - 1)
+            take_min(0, c)
+            if c > 0:
+                quantize_part(c - 1)
+            for t in range(1, PACK):
+                take_min(t, c)
+            nc.sync.dma_start(out_rows[:, :, c * PART : (c + 1) * PART], low[c][:])
+        round_part(PARTS - 1)
+        quantize_part(PARTS - 1)
+        for q in range(QUADS):
+            queue = nc.sync if q % 2 == 0 else nc.scalar
+            queue.dma_start(out_2[0, 4 * q : 4 * q + 4, :].bitcast(I32), out_scales[32 * q : 32 * q + 4, :].bitcast(I32))

@@ -22,7 +22,8 @@ BANK = 512
 PART = 256
 PARTS = U // PART
 ORDER = (0, 2, 3, 1)
-W2_ROW = 4
+PIECES = ((0, 512), (512, 256), (768, 256))
+VECTOR_PARTS = 2
 
 
 def tile_picked_pagemin_none_po_kernel(
@@ -35,7 +36,6 @@ def tile_picked_pagemin_none_po_kernel(
 
     with ExitStack() as ctx:
         keep = ctx.enter_context(tc.tile_pool(name="keep", bufs=1))
-        ring = ctx.enter_context(tc.tile_pool(name="ring", bufs=2))
         psum = ctx.enter_context(tc.psum_pool(name="psum", bufs=8))
 
         offs_sb = keep.tile([P, S // 16], U16, name="offs_sb")
@@ -44,12 +44,12 @@ def tile_picked_pagemin_none_po_kernel(
         first, second, third, last = ORDER
         x_tab = keep.tile([P, T], U32, name="x_tab", tag="x_then_page", align_bytes=64)
         xs_tab = keep.tile([P, T], U8, name="xs_tab", tag="xs_then_page", align_bytes=64)
-        w1_raw = keep.tile([P, H], U32, name="w1_raw", tag="w1_then_page", align_bytes=64)
-        ws_raw = keep.tile([P, H], U8, name="ws_raw", tag="ws_then_gain", align_bytes=64)
-        page = {first: keep.tile([P, U], F32, name="page_first", align_bytes=64)}
+        w1_raw = keep.tile([P, H], U32, name="w1_raw", tag="w1_then_gain", align_bytes=64)
+        ws_raw = keep.tile([P, H], U8, name="ws_raw", tag="ws_then_page", align_bytes=64)
+        page = {first: keep.tile([P, U], F32, name="page_first", tag="page_then_gate", align_bytes=64)}
         mem_rows = mem.rearrange("(p t) w -> p t w", t=PACK)
 
-        nc.vector.memset(xs_tab[:].bitcast(I32), 0)
+        nc.gpsimd.memset(xs_tab[:].bitcast(I32), 0)
         nc.vector.memset(ws_raw[:].bitcast(I32), 0)
 
         def load_scale_rows(queue, plane, scales, q):
@@ -58,13 +58,13 @@ def tile_picked_pagemin_none_po_kernel(
         nc.sync.dma_start(offs_sb[:], offs)
         nc.sync.dma_start(slot_sb[:], slot)
         nc.sync.dma_start(mate_sb[:], mate)
+        for q in range(QUADS):
+            load_scale_rows(nc.sync, xs_tab, x_scales, q)
         nc.sync.dma_start(x_tab[:].bitcast(I32), words_of(x_words))
+        for q in range(QUADS):
+            load_scale_rows(nc.sync, ws_raw, w1_scales, q)
         nc.sync.dma_start(w1_raw[:].bitcast(I32), words_of(w1_words))
         nc.sync.dma_start(page[first][:], mem_rows[:, first, :])
-        for q in range(QUADS):
-            load_scale_rows(nc.scalar, xs_tab, x_scales, q)
-        for q in range(QUADS):
-            load_scale_rows(nc.scalar if q < QUADS // 2 else nc.gpsimd, ws_raw, w1_scales, q)
 
         xq = keep.tile([P, S], U32, name="xq", tag=f"old{last}", align_bytes=64)
         xq_s = keep.tile([P, S], U8, name="xq_s", tag="xq_s_then_ws2", align_bytes=64)
@@ -77,15 +77,12 @@ def tile_picked_pagemin_none_po_kernel(
             return dealt
 
         ws = deal(nc.vector.tensor_copy, ws_raw, U8, "ws", "ws")
-        w1 = keep.tile([P, PACK, P], U32, name="w1", tag=f"old{third}", align_bytes=64)
-        w1_by_plane = w1_raw[:].rearrange("p (m t) -> p t m", t=PACK)
-        for t in ORDER:
-            nc.gpsimd.tensor_copy(w1[:, t, :], w1_by_plane[:, t, :])
+        w1 = deal(nc.vector.tensor_copy, w1_raw, U32, "w1", f"old{third}")
 
-        for t, tag in ((second, "xs_then_page"), (third, "w1_then_page"), (last, "x_then_page")):
+        for t, tag in ((second, "xs_then_page"), (third, "x_then_page"), (last, "ws_then_page")):
             page[t] = keep.tile([P, U], F32, name=f"page{t}", tag=tag, align_bytes=64)
             nc.sync.dma_start(page[t][:], mem_rows[:, t, :])
-        gain = keep.tile([P, PACK], F32, name="gain", tag="ws_then_gain", align_bytes=64)
+        gain = keep.tile([P, PACK], F32, name="gain", tag="w1_then_gain", align_bytes=64)
         nc.sync.dma_start(gain[:], gn.rearrange("(p t) o -> p (t o)", t=PACK))
 
         y = {}
@@ -93,7 +90,7 @@ def tile_picked_pagemin_none_po_kernel(
             cols = slice(t * P, (t + 1) * P)
             y[t] = psum.tile([P, BANK], F32, name="bank")
             nc.tensor.matmul_mx(
-                out=y[t][:], lhsT=w1[:, t, :].bitcast(FP8X4), lhsT_scale=ws[:, cols],
+                out=y[t][:], lhsT=w1[:, cols].bitcast(FP8X4), lhsT_scale=ws[:, cols],
                 rhs=xq[:].bitcast(FP8X4), rhs_scale=xq_s[:], start=True, stop=True,
             )
 
@@ -115,7 +112,7 @@ def tile_picked_pagemin_none_po_kernel(
                 nc.scalar.activation(old[t][:], page[t][:].indirect(slot_sb[:]), ACT.Copy)
 
         def make_gate(t):
-            gate[t] = ring.tile([P, S], F32, name="gate", align_bytes=64)
+            gate[t] = keep.tile([P, S], F32, name="gate", tag="page_then_gate" if t == last else f"gate{t}", align_bytes=64)
             nc.scalar.activation(gate[t][:], y[t][:], ACT.Sigmoid)
 
         def make_diff(t):
@@ -136,9 +133,10 @@ def tile_picked_pagemin_none_po_kernel(
         make_diff(first)
         scatter(first)
         make_gate(second)
-        for t in ORDER[1:]:
-            fetch_old(t)
+        fetch_old(second)
         make_gate(third)
+        fetch_old(third)
+        fetch_old(last)
         make_diff(second)
         make_diff(third)
         for c in range(PARTS):
@@ -154,9 +152,9 @@ def tile_picked_pagemin_none_po_kernel(
         scatter(last)
         for c in range(PARTS):
             scale_on_scalar(third, c)
-        for c in range(PARTS // 2):
+        for c in range(VECTOR_PARTS):
             scale_on_vector(last, c)
-        for c in range(PARTS // 2, PARTS):
+        for c in range(VECTOR_PARTS, PARTS):
             scale_on_scalar(last, c)
 
         z_codes, z_scales = [], []
@@ -194,41 +192,45 @@ def tile_picked_pagemin_none_po_kernel(
         low, rounded = {}, {}
 
         def take_min(t, c):
-            half, i = divmod(c, BANK // PART)
-            mated = ring.tile([P, PART], F32, name=f"mated{t}", bufs=PARTS, align_bytes=64)
-            window = h[t][:].indirect(mate_sb[:, c * PART // 16 : (c + 1) * PART // 16])
+            start, n = PIECES[c]
+            half, at = divmod(start, BANK)
+            mated = keep.tile([P, n], F32, name=f"mated{t}_{c}", align_bytes=64)
+            window = h[t][:].indirect(mate_sb[:, start // 16 : (start + n) // 16])
             if (t, c) == (0, 0):
                 nc.vector.tensor_copy(mated[:], window)
             else:
                 nc.scalar.activation(mated[:], window, ACT.Copy)
-            nc.vector.tensor_tensor(low[c][:, t, :], h_bank[t, half][:, i * PART : (i + 1) * PART], mated[:], ALU.min)
+            nc.vector.tensor_tensor(low[c][:, t, :], h_bank[t, half][:, at : at + n], mated[:], ALU.min)
 
         def round_part(c):
-            rounded[c] = keep.tile([P, PART, PACK], BF16, name=f"rounded{c}", align_bytes=64)
+            rounded[c] = keep.tile([P, PIECES[c][1], PACK], BF16, name=f"rounded{c}", align_bytes=64)
             nc.vector.tensor_copy(
                 rounded[c][:].rearrange("p (g i) t -> p g t i", i=4), low[c][:].rearrange("p t (g i) -> p g t i", i=4)
             )
 
         def quantize_part(c):
-            cols = slice(c * PART, (c + 1) * PART)
-            codes = keep.tile([P, PART], U32, name=f"codes{c}", align_bytes=64)
+            start, n = PIECES[c]
+            codes = keep.tile([P, n], U32, name=f"codes{c}", align_bytes=64)
             nc.vector.quantize_mx(
-                out=codes[:].bitcast(FP8X4), scales=out_scales[:, cols], in_=rounded[c][:].rearrange("p w t -> p (w t)")
+                out=codes[:].bitcast(FP8X4), scales=out_scales[:, start : start + n],
+                in_=rounded[c][:].rearrange("p w t -> p (w t)"),
             )
-            nc.sync.dma_start(out_words[:, cols], codes[:].bitcast(I32))
+            nc.sync.dma_start(out_words[:, start : start + n], codes[:].bitcast(I32))
 
-        for c in range(PARTS):
-            low[c] = keep.tile([P, PACK, PART], F32, name=f"low{c}", tag=f"low{c}", align_bytes=64)
+        for c, (start, n) in enumerate(PIECES):
+            low[c] = keep.tile([P, PACK, n], F32, name=f"low{c}", tag=f"low{c}", align_bytes=64)
             if c > 0:
                 round_part(c - 1)
             take_min(0, c)
             if c > 0:
                 quantize_part(c - 1)
-            for t in range(1, PACK):
+            for t in range(1, PACK - 1):
                 take_min(t, c)
-            nc.sync.dma_start(out_rows[:, :, c * PART : (c + 1) * PART], low[c][:])
-        round_part(PARTS - 1)
-        quantize_part(PARTS - 1)
+            nc.sync.dma_start(out_rows[:, : PACK - 1, start : start + n], low[c][:, : PACK - 1, :])
+            take_min(PACK - 1, c)
+            nc.sync.dma_start(out_rows[:, PACK - 1, start : start + n], low[c][:, PACK - 1, :])
+        round_part(len(PIECES) - 1)
+        quantize_part(len(PIECES) - 1)
         for q in range(QUADS):
             queue = nc.sync if q % 2 == 0 else nc.scalar
             queue.dma_start(out_2[0, 4 * q : 4 * q + 4, :].bitcast(I32), out_scales[32 * q : 32 * q + 4, :].bitcast(I32))

from contextlib import ExitStack

import concourse.mybir as mybir

K, T, S, N, H, U = 512, 2048, 512, 512, 512, 1024
FLOPS = 2 * K * H * S + 2 * H * N * U

F32 = mybir.dt.float32
BF16 = mybir.dt.bfloat16
I32 = mybir.dt.int32
U32 = mybir.dt.uint32
U16 = mybir.dt.uint16
U8 = mybir.dt.uint8
FP8X4 = mybir.dt.float8_e4m3fn_x4
ACT = mybir.ActivationFunctionType
ALU = mybir.AluOpType

P = 128
PACK = 4
QUADS = 4
BANK = 512
PART = 256
PARTS = U // PART
ORDER = (0, 2, 3, 1)
PIECES = ((0, 512), (512, 256), (768, 256))
VECTOR_PARTS = 2


def tile_picked_pagemin_none_po_kernel(
    tc, x_words, x_scales, w1_words, w1_scales, mem, gn, w2_words, w2_scales, offs, slot, mate, out_0, out_1, out_2
):
    nc = tc.nc

    def words_of(dram):
        return dram[0].rearrange("p n t -> p (n t)").bitcast(I32)

    with ExitStack() as ctx:
        keep = ctx.enter_context(tc.tile_pool(name="keep", bufs=1))
        psum = ctx.enter_context(tc.psum_pool(name="psum", bufs=8))

        offs_sb = keep.tile([P, S // 16], U16, name="offs_sb")
        slot_sb = keep.tile([P, S // 16], U16, name="slot_sb")
        mate_sb = keep.tile([P, U // 16], U16, name="mate_sb")
        first, second, third, last = ORDER
        x_tab = keep.tile([P, T], U32, name="x_tab", tag="x_then_page", align_bytes=64)
        xs_tab = keep.tile([P, T], U8, name="xs_tab", tag="xs_then_page", align_bytes=64)
        w1_raw = keep.tile([P, H], U32, name="w1_raw", tag="w1_then_gain", align_bytes=64)
        ws_raw = keep.tile([P, H], U8, name="ws_raw", tag="ws_then_page", align_bytes=64)
        page = {first: keep.tile([P, U], F32, name="page_first", tag="page_then_gate", align_bytes=64)}
        mem_rows = mem.rearrange("(p t) w -> p t w", t=PACK)

        nc.gpsimd.memset(xs_tab[:].bitcast(I32), 0)
        nc.vector.memset(ws_raw[:].bitcast(I32), 0)

        def load_scale_rows(queue, plane, scales, q):
            queue.dma_start(plane[32 * q : 32 * q + 4, :].bitcast(I32), scales[0, 4 * q : 4 * q + 4, :].bitcast(I32))

        nc.sync.dma_start(offs_sb[:], offs)
        nc.sync.dma_start(slot_sb[:], slot)
        nc.sync.dma_start(mate_sb[:], mate)
        for q in range(QUADS):
            load_scale_rows(nc.sync, xs_tab, x_scales, q)
        nc.sync.dma_start(x_tab[:].bitcast(I32), words_of(x_words))
        for q in range(QUADS):
            load_scale_rows(nc.sync, ws_raw, w1_scales, q)
        nc.sync.dma_start(w1_raw[:].bitcast(I32), words_of(w1_words))
        nc.sync.dma_start(page[first][:], mem_rows[:, first, :])

        xq = keep.tile([P, S], U32, name="xq", tag=f"old{last}", align_bytes=64)
        xq_s = keep.tile([P, S], U8, name="xq_s", tag="xq_s_then_ws2", align_bytes=64)
        nc.vector.tensor_copy(xq_s[:], xs_tab[:].indirect(offs_sb[:]))
        nc.vector.tensor_copy(xq[:], x_tab[:].indirect(offs_sb[:]))

        def deal(copy, raw, dtype, name, tag):
            dealt = keep.tile([P, H], dtype, name=name, tag=tag, align_bytes=64)
            copy(dealt[:].rearrange("p (t m) -> p m t", t=PACK), raw[:].rearrange("p (m t) -> p m t", t=PACK))
            return dealt

        ws = deal(nc.vector.tensor_copy, ws_raw, U8, "ws", "ws")
        w1 = deal(nc.vector.tensor_copy, w1_raw, U32, "w1", f"old{third}")

        for t, tag in ((second, "xs_then_page"), (third, "x_then_page"), (last, "ws_then_page")):
            page[t] = keep.tile([P, U], F32, name=f"page{t}", tag=tag, align_bytes=64)
            nc.sync.dma_start(page[t][:], mem_rows[:, t, :])
        gain = keep.tile([P, PACK], F32, name="gain", tag="w1_then_gain", align_bytes=64)
        nc.sync.dma_start(gain[:], gn.rearrange("(p t) o -> p (t o)", t=PACK))

        y = {}
        for t in ORDER:
            cols = slice(t * P, (t + 1) * P)
            y[t] = psum.tile([P, BANK], F32, name="bank")
            nc.tensor.matmul_mx(
                out=y[t][:], lhsT=w1[:, cols].bitcast(FP8X4), lhsT_scale=ws[:, cols],
                rhs=xq[:].bitcast(FP8X4), rhs_scale=xq_s[:], start=True, stop=True,
            )

        w2_raw = keep.tile([P, N], U32, name="w2_raw", tag="ws", align_bytes=64)
        nc.sync.dma_start(w2_raw[:].bitcast(I32), words_of(w2_words))
        ws2_raw = keep.tile([P, H], U8, name="ws2_raw", tag="xq_s_then_ws2", align_bytes=64)
        nc.gpsimd.memset(ws2_raw[:].bitcast(I32), 0)
        for q in range(QUADS):
            load_scale_rows(nc.sync, ws2_raw, w2_scales, q)

        z = [keep.tile([P, PART, PACK], BF16, name=f"z{c}", align_bytes=64) for c in range(PARTS)]
        old, gate, diff = {}, {}, {}

        def fetch_old(t):
            old[t] = keep.tile([P, S], F32, name=f"old{t}", tag=f"old{first if t == second else t}", align_bytes=64)
            if t == first:
                nc.vector.tensor_copy(old[t][:], page[t][:].indirect(slot_sb[:]))
            else:
                nc.scalar.activation(old[t][:], page[t][:].indirect(slot_sb[:]), ACT.Copy)

        def make_gate(t):
            gate[t] = keep.tile([P, S], F32, name="gate", tag="page_then_gate" if t == last else f"gate{t}", align_bytes=64)
            nc.scalar.activation(gate[t][:], y[t][:], ACT.Sigmoid)

        def make_diff(t):
            diff[t] = keep.tile([P, S], F32, name=f"diff{t}", tag=f"diff{t}", align_bytes=64)
            nc.vector.tensor_tensor(diff[t][:], y[t][:], old[t][:], ALU.subtract)

        def scatter(t):
            nc.vector.tensor_tensor(page[t][:].indirect(slot_sb[:]), gate[t][:], diff[t][:], ALU.mult)

        def scale_on_scalar(t, c):
            nc.scalar.activation(z[c][:, :, t], page[t][:, c * PART : (c + 1) * PART], ACT.Copy, scale=gain[:, t : t + 1])

        def scale_on_vector(t, c):
            nc.vector.tensor_scalar(z[c][:, :, t], page[t][:, c * PART : (c + 1) * PART], gain[:, t : t + 1], None, ALU.mult)

        fetch_old(first)
        make_gate(first)
        make_diff(first)
        scatter(first)
        make_gate(second)
        fetch_old(second)
        make_gate(third)
        fetch_old(third)
        fetch_old(last)
        make_diff(second)
        make_diff(third)
        for c in range(PARTS):
            scale_on_scalar(first, c)
        scatter(second)
        make_gate(last)
        for c in range(PARTS):
            scale_on_scalar(second, c)
        scatter(third)
        make_diff(last)
        w2 = deal(nc.vector.tensor_copy, w2_raw, U32, "w2", f"diff{second}")
        ws2 = deal(nc.vector.tensor_copy, ws2_raw, U8, "ws2", f"diff{third}")
        scatter(last)
        for c in range(PARTS):
            scale_on_scalar(third, c)
        for c in range(VECTOR_PARTS):
            scale_on_vector(last, c)
        for c in range(VECTOR_PARTS, PARTS):
            scale_on_scalar(last, c)

        z_codes, z_scales = [], []
        for c in range(PARTS):
            z_codes.append(keep.tile([P, PART], U32, name=f"z_codes{c}", tag=f"low{PARTS - 1 - c}", align_bytes=64))
            z_scales.append(keep.tile([P, PART], U8, name=f"z_scales{c}", align_bytes=64))
            nc.vector.quantize_mx(
                out=z_codes[c][:].bitcast(FP8X4), scales=z_scales[c][:], in_=z[c][:].rearrange("p w t -> p (w t)")
            )

        h_bank, h = {}, []
        for t in range(PACK):
            cols = slice(t * P, (t + 1) * P)
            for half in range(U // BANK):
                h_bank[t, half] = psum.tile([P, BANK], F32, name="bank")
                for i in range(BANK // PART):
                    c = half * (BANK // PART) + i
                    nc.tensor.matmul_mx(
                        out=h_bank[t, half][:, i * PART : (i + 1) * PART], lhsT=w2[:, cols].bitcast(FP8X4),
                        lhsT_scale=ws2[:, cols], rhs=z_codes[c][:].bitcast(FP8X4), rhs_scale=z_scales[c][:],
                        start=True, stop=True,
                    )
        for t in range(PACK):
            h.append(keep.tile([P, U], F32, name=f"h{t}", align_bytes=64))
            for half in range(U // BANK):
                dst = h[t][:, half * BANK : (half + 1) * BANK]
                if half == 0:
                    nc.scalar.copy(dst, h_bank[t, half][:])
                else:
                    nc.vector.tensor_copy(dst, h_bank[t, half][:])

        out_rows = out_0.rearrange("(p t) w -> p t w", t=PACK)
        out_words = words_of(out_1)
        out_scales = keep.tile([P, U], U8, name="out_scales", align_bytes=64)
        low, rounded = {}, {}

        def take_min(t, c):
            start, n = PIECES[c]
            half, at = divmod(start, BANK)
            mated = keep.tile([P, n], F32, name=f"mated{t}_{c}", align_bytes=64)
            window = h[t][:].indirect(mate_sb[:, start // 16 : (start + n) // 16])
            if (t, c) == (0, 0):
                nc.vector.tensor_copy(mated[:], window)
            else:
                nc.scalar.activation(mated[:], window, ACT.Copy)
            nc.vector.tensor_tensor(low[c][:, t, :], h_bank[t, half][:, at : at + n], mated[:], ALU.min)

        def round_part(c):
            rounded[c] = keep.tile([P, PIECES[c][1], PACK], BF16, name=f"rounded{c}", align_bytes=64)
            nc.vector.tensor_copy(
                rounded[c][:].rearrange("p (g i) t -> p g t i", i=4), low[c][:].rearrange("p t (g i) -> p g t i", i=4)
            )

        def quantize_part(c):
            start, n = PIECES[c]
            codes = keep.tile([P, n], U32, name=f"codes{c}", align_bytes=64)
            nc.vector.quantize_mx(
                out=codes[:].bitcast(FP8X4), scales=out_scales[:, start : start + n],
                in_=rounded[c][:].rearrange("p w t -> p (w t)"),
            )
            nc.sync.dma_start(out_words[:, start : start + n], codes[:].bitcast(I32))

        for c, (start, n) in enumerate(PIECES):
            low[c] = keep.tile([P, PACK, n], F32, name=f"low{c}", tag=f"low{c}", align_bytes=64)
            if c > 0:
                round_part(c - 1)
            take_min(0, c)
            if c > 0:
                quantize_part(c - 1)
            for t in range(1, PACK - 1):
                take_min(t, c)
            nc.sync.dma_start(out_rows[:, : PACK - 1, start : start + n], low[c][:, : PACK - 1, :])
            take_min(PACK - 1, c)
            nc.sync.dma_start(out_rows[:, PACK - 1, start : start + n], low[c][:, PACK - 1, :])
        round_part(len(PIECES) - 1)
        quantize_part(len(PIECES) - 1)
        for q in range(QUADS):
            queue = nc.sync if q % 2 == 0 else nc.scalar
            queue.dma_start(out_2[0, 4 * q : 4 * q + 4, :].bitcast(I32), out_scales[32 * q : 32 * q + 4, :].bitcast(I32))
